import numpy as np
import ml_dtypes


def mxq(x, axis, fmt="e4m3"):
    dtype, down = {"e4m3": (ml_dtypes.float8_e4m3fn, 7), "e5m2": (ml_dtypes.float8_e5m2, 14)}[fmt]
    v = np.moveaxis(np.asarray(x, np.float32).astype(ml_dtypes.bfloat16).astype(np.float64), axis, -1)
    blocks = v.reshape(v.shape[:-1] + (-1, 32))
    amax = np.abs(blocks).max(-1, keepdims=True)
    byte = np.maximum(np.where(amax > 0, np.frexp(amax)[1] - 1 + 127, 0) - down, 1)
    scale = np.exp2(byte - 127.0)
    codes = (blocks / scale).astype(np.float32).astype(dtype).astype(np.float64)
    return np.moveaxis((codes * scale).reshape(v.shape), -1, axis)


WIDE = False


def mx_kscale(k):
    if not WIDE:
        return np.ones(k)
    levels = np.array([10, -10, 5, -5, 0])
    if k % 512:
        return np.exp2(np.random.permutation(np.resize(levels, k // 32))).repeat(32)
    a = np.empty((k // 512, 16))
    for p in range(k // 512):
        a[p, :8] = np.random.permutation(np.resize(levels, 8))
        for g in range(8):
            far = levels[np.abs(levels - a[p, g]) >= 10]
            a[p, g + 8] = far[np.random.randint(len(far))]
    return np.exp2(a.ravel()).repeat(32)


def f64(x):
    return np.asarray(x).astype(np.float64)


def striped(idx):
    return np.tile(idx.reshape(-1, 16).T, (8, 1)).astype(np.uint16)


def unstriped(offs):
    return offs[:16].T.reshape(-1).astype(np.int64)


def pack_weight(w):
    k, n = w.shape
    w = f64(np.asarray(w, np.float32).astype(ml_dtypes.bfloat16)).reshape(k // 32, 32, n)
    amax = np.abs(w).max(1)
    byte = np.clip(np.where(amax > 0, np.frexp(amax)[1] - 1 + 127 - 7, 1), 1, 254)
    scaled = (w * np.exp2(127.0 - byte)[:, None, :]).reshape(k, n).astype(np.float32)
    words = np.ascontiguousarray(scaled.reshape(k // 512, 128, 4, n).transpose(0, 1, 3, 2)).astype(ml_dtypes.float8_e4m3fn).view(np.uint8)
    return words, np.ascontiguousarray(byte.astype(np.uint8).reshape(k // 512, 16, n))


def unpack_weight(words, scales):
    g, p, n, _ = words.shape
    vals = np.ascontiguousarray(words).view(ml_dtypes.float8_e4m3fn).astype(np.float64) * np.repeat(np.exp2(scales.astype(np.float64) - 127.0), 8, axis=1)[..., None]
    return vals.transpose(0, 1, 3, 2).reshape(g * 512, n)


K, T, S, D, N = 512, 2048, 1024, 4, 256
P = 2 ** 7


def setup_inputs():
    n = np.random.standard_normal
    s = mx_kscale(K)[:, None]
    packed_xT = pack_weight(n((K, T)) * s)
    return {
        "x_words": packed_xT[0],
        "x_scales": packed_xT[1],
        "w1": (n((K, N)) / np.sqrt(K) / s).astype(np.float32),
        "w2": (n((K, N)) / np.sqrt(K) / s).astype(np.float32),
        "w3": (n((K, N)) / np.sqrt(K) / s).astype(np.float32),
        "vis": (np.tile(np.random.uniform(0.0, 1.0, S), (P, 1))).astype(np.float32),
        "offs": striped(np.random.permutation(T)[:S]),
    }


def reference(x_words, x_scales, w1, w2, w3, vis, offs):
    xq = unpack_weight(x_words, x_scales)[:, unstriped(offs)]
    yp = mxq(f64(w2), 0, "e4m3").T @ xq
    pdfa = np.log(np.exp(yp) + 1.0) + 0.2
    yq = mxq(f64(w3), 0, "e4m3").T @ xq
    pdfb = np.log(np.exp(yq) + 1.0) + 0.2
    wt = ((pdfa) ** 2) / ((pdfa) ** 2 + (pdfb) ** 2)
    yf = mxq(f64(w1), 0, "e4m3").T @ xq
    con = np.exp(0.6 * yf)
    est = (f64(vis)[:1] * wt) * (con / pdfa)
    return est.reshape(len(est), -1, D).mean(axis=2)

@@ -1,0 +1,199 @@
+import math
+from contextlib import ExitStack
+
+import concourse.mybir as mybir
+from concourse.masks import make_identity
+
+K, T, S, D, N = 512, 2048, 1024, 4, 256
+P = 128
+FLOPS = 3 * 2 * K * N * S
+
+F32 = mybir.dt.float32
+BF16 = mybir.dt.bfloat16
+I32 = mybir.dt.int32
+U32 = mybir.dt.uint32
+U16 = mybir.dt.uint16
+U8 = mybir.dt.uint8
+FP8X4 = mybir.dt.float8_e4m3fn_x4
+ACT = mybir.ActivationFunctionType
+ALU = mybir.AluOpType
+
+BLOCK = P * D
+BLOCKS = S // BLOCK
+UNITS = [(b, h) for b in range(BLOCKS) for h in range(2)]
+FLOOR = 0.2
+TINY = 2.0 ** -60
+
+
+def tile_picked_ymisw_pow_p_kernel(tc, x_words, x_scales, w1, w2, w3, vis, offs, out):
+    nc = tc.nc
+    with ExitStack() as ctx:
+        pool = ctx.enter_context(tc.tile_pool(name="sbuf", bufs=1))
+        psum = ctx.enter_context(tc.psum_pool(name="psum", bufs=1))
+
+        def sb(name, shape, dtype):
+            return pool.tile(shape, dtype, name=name, align_bytes=64)
+
+        offsets = sb("offsets", [P, S // 16], U16)
+        words = sb("words", [P, T], U32)
+        scales = sb("scales", [P, T], U8)
+        raw = {k: sb("raw_" + k, [P, 4, N], F32) for k in ("q", "p", "f")}
+        seen = sb("seen", [P, BLOCKS, D], F32)
+
+        nc.sync.dma_start(offsets[:], offs)
+        scale_rows = x_scales[0].bitcast(I32)
+        for q in range(4):
+            nc.sync.dma_start(
+                out=scales[32 * q : 32 * q + 32, :].bitcast(I32),
+                in_=scale_rows[4 * q : 4 * q + 4, :].unsqueeze(0).broadcast_to([8, 4, T // 4]),
+            )
+        nc.sync.dma_start(out=words[:].bitcast(I32), in_=x_words[0].rearrange("p n t -> p (n t)").bitcast(I32))
+        for k, w in (("q", w3), ("p", w2), ("f", w1)):
+            nc.sync.dma_start(out=raw[k][:], in_=w.rearrange("(p j) n -> p j n", j=4))
+        nc.sync.dma_start(out=seen[:], in_=vis[0:1, :].rearrange("o (b p d) -> p (o b) d", p=P, d=D))
+
+        warm = sb("warm", [P, 1], F32)
+        warm2 = sb("warm2", [P, 1], F32)
+        nc.vector.memset(warm[:], 0.0)
+        nc.scalar.activation(out=warm2[:], in_=warm[:], func=ACT.Sigmoid)
+
+        ident = sb("ident", [P, P], F32)
+        make_identity(nc, ident[:])
+
+        x_codes = [sb("x_codes%d" % b, [P, BLOCK], U32) for b in range(BLOCKS)]
+        x_listed = [sb("x_listed%d" % b, [P, BLOCK], U8) for b in range(BLOCKS)]
+        x_bytes = [sb("x_bytes%d" % b, [P, BLOCK], U8) for b in range(BLOCKS)]
+        w_bf = {k: sb("w_bf_" + k, [P, N, 4], BF16) for k in raw}
+        w_codes = {k: sb("w_codes_" + k, [P, N], U32) for k in raw}
+        w_bytes = {k: sb("w_bytes_" + k, [P, N], U8) for k in raw}
+
+        def entries(b):
+            return offsets[:, b * BLOCK // 16 : (b + 1) * BLOCK // 16]
+
+        def gather_bytes(b):
+            nc.vector.tensor_copy(x_listed[b][:], scales[:].indirect(entries(b)))
+            nc.vector.tensor_copy(
+                x_bytes[b][:].rearrange("p (d v) -> p d v", d=D),
+                x_listed[b][:].rearrange("p (v d) -> p d v", d=D),
+            )
+
+        def gather_words(b):
+            nc.vector.tensor_copy(x_codes[b][:].rearrange("p (d v) -> p v d", d=D), words[:].indirect(entries(b)))
+
+        def views(k):
+            return (w_bf[k][:].rearrange("p (c i) t -> p c t i", i=4), raw[k][:].rearrange("p t (c i) -> p c t i", i=4))
+
+        def quantise(k):
+            nc.vector.quantize_mx(
+                out=w_codes[k][:].bitcast(FP8X4),
+                scales=w_bytes[k][:],
+                in_=w_bf[k][:].rearrange("p n t -> p (n t)"),
+            )
+
+        banks = {(k, u): psum.tile([P, 2 * N], F32, name="bank_%s%d" % (k, u)) for k in ("p", "q") for u in range(4)}
+
+        def product(k, u, bank):
+            b, h = UNITS[u]
+            for i in range(2):
+                cols = slice((2 * h + i) * P, (2 * h + i + 1) * P)
+                nc.tensor.matmul_mx(
+                    out=bank[:, i * N : (i + 1) * N],
+                    lhsT=x_codes[b][:, cols].bitcast(FP8X4),
+                    lhsT_scale=x_bytes[b][:, cols],
+                    rhs=w_codes[k][:].bitcast(FP8X4),
+                    rhs_scale=w_bytes[k][:],
+                    start=True,
+                    stop=True,
+                )
+
+        sig = [sb("sig%d" % u, [P, 2, 2 * N], F32) for u in range(4)]
+        side = {"p": 0, "q": 1}
+
+        def sigmoid(k, u):
+            product(k, u, banks[k, u])
+            nc.scalar.activation(out=sig[u][:, side[k], :], in_=banks[k, u][:], func=ACT.Sigmoid)
+
+        gather_bytes(0)
+        gather_bytes(1)
+        gather_words(0)
+        dst, src = views("q")
+        nc.scalar.activation(out=dst, in_=src, func=ACT.Copy, scale=-1.0)
+        quantise("q")
+        dst, src = views("p")
+        nc.vector.tensor_scalar(out=dst, in0=src, scalar1=-1.0, scalar2=None, op0=ALU.mult)
+        sigmoid("q", 0)
+        sigmoid("q", 1)
+        quantise("p")
+        gather_words(1)
+        sigmoid("p", 0)
+        sigmoid("p", 1)
+        for u in (2, 3):
+            sigmoid("q", u)
+        for u in (2, 3):
+            sigmoid("p", u)
+        dst, src = views("f")
+        nc.vector.tensor_copy(out=dst, in_=src)
+        quantise("f")
+
+        logs = [sb("logs%d" % u, [P, 2, 2 * N], F32) for u in range(4)]
+        neg_a = sb("neg_a", [P, 8, N], F32)
+        neg_b = [sb("neg_b%d" % u, [P, 2 * N], F32) for u in range(4)]
+        sq_a = [sb("sq_a%d" % u, [P, 2 * N], F32) for u in range(4)]
+        sq_b = [sb("sq_b%d" % u, [P, 2 * N], F32) for u in range(4)]
+        den = [sb("den%d" % u, [P, 2 * N], F32) for u in range(4)]
+        log_den = [sb("log_den%d" % u, [P, 2 * N], F32) for u in range(4)]
+        expo = sb("expo", [P, 8, N], F32)
+
+        def unit(t, u):
+            return t[:, 2 * u : 2 * u + 2, :].rearrange("p i n -> p (i n)")
+
+        def stage_log(u):
+            c = math.e ** -FLOOR
+            nc.scalar.activation(out=logs[u][:], in_=sig[u][:], func=ACT.Ln, scale=c, bias=c * TINY)
+
+        def stage_min(u):
+            nc.vector.scalar_tensor_tensor(
+                out=neg_b[u][:], in0=banks["q", u][:], scalar=-FLOOR, in1=logs[u][:, 1, :], op0=ALU.add, op1=ALU.min
+            )
+            nc.vector.scalar_tensor_tensor(
+                out=unit(neg_a, u), in0=banks["p", u][:], scalar=-FLOOR, in1=logs[u][:, 0, :], op0=ALU.add, op1=ALU.min
+            )
+            product("f", u, banks["p", u])
+
+        def stage_den(u):
+            nc.scalar.activation(out=sq_b[u][:], in_=neg_b[u][:], func=ACT.Square)
+            nc.vector.tensor_tensor(out=sq_a[u][:], in0=unit(neg_a, u), in1=unit(neg_a, u), op=ALU.mult)
+            nc.vector.tensor_tensor(out=den[u][:], in0=sq_a[u][:], in1=sq_b[u][:], op=ALU.add)
+
+        def stage_expo(u):
+            nc.scalar.activation(out=log_den[u][:], in_=den[u][:], func=ACT.Ln)
+            nc.vector.scalar_tensor_tensor(
+                out=unit(expo, u), in0=banks["p", u][:], scalar=0.6, in1=log_den[u][:], op0=ALU.mult, op1=ALU.subtract
+            )
+
+        stages = (stage_log, stage_min, stage_den, stage_expo)
+        for step in range(4 + len(stages) - 1):
+            for s, stage in enumerate(stages):
+                if 0 <= step - s < 4:
+                    stage(step - s)
+
+        for m in range(2):
+            cols = slice(m * P, (m + 1) * P)
+            result = sb("result%d" % m, [P, BLOCKS, P], F32)
+            for c in range(2):
+                ratio = sb("ratio%d%d" % (m, c), [P, 4, P], F32)
+                est = sb("est%d%d" % (m, c), [P, 4, P], F32)
+                nc.scalar.activation(out=ratio[:], in_=expo[:, c:8:2, cols], func=ACT.Exp)
+                for u, (b, h) in enumerate(UNITS):
+                    d = 2 * h + c
+                    nc.vector.scalar_tensor_tensor(
+                        out=est[:, u, :], in0=ratio[:, u, :], scalar=seen[:, b, d : d + 1], in1=neg_a[:, 2 * u + c, cols],
+                        op0=ALU.mult, op1=ALU.mult,
+                    )
+                    nc.tensor.matmul(
+                        banks["q", 2 * m + b][:, 0:P], lhsT=est[:, u, :], rhs=ident[:],
+                        start=(c == 0 and h == 0), stop=(c == 1 and h == 1), is_transpose=True,
+                    )
+            for b in range(BLOCKS):
+                nc.scalar.activation(out=result[:, b, :], in_=banks["q", 2 * m + b][:, 0:P], func=ACT.Copy, scale=-1.0 / D)
+            nc.sync.dma_start(out=out[cols, :], in_=result[:].rearrange("p b v -> p (b v)"))

@@ -18,11 +18,14 @@ FP8X4 = mybir.dt.float8_e4m3fn_x4
 ACT = mybir.ActivationFunctionType
 ALU = mybir.AluOpType
 
+PACK = 4
 BLOCK = P * D
 BLOCKS = S // BLOCK
-UNITS = [(b, h) for b in range(BLOCKS) for h in range(2)]
+PAIRS = S // (2 * P)
+SIDES = ("b", "a")
 FLOOR = 0.2
-TINY = 2.0 ** -60
+GAIN = math.e**FLOOR
+CAP = 2.0**60
 
 
 def tile_picked_ymisw_pow_p_kernel(tc, x_words, x_scales, w1, w2, w3, vis, offs, out):
@@ -31,71 +34,67 @@ def tile_picked_ymisw_pow_p_kernel(tc, x_words, x_scales, w1, w2, w3, vis, offs,
         pool = ctx.enter_context(tc.tile_pool(name="sbuf", bufs=1))
         psum = ctx.enter_context(tc.psum_pool(name="psum", bufs=1))
 
-        def sb(name, shape, dtype):
-            return pool.tile(shape, dtype, name=name, align_bytes=64)
+        def sb(name, shape, dtype, tag=None):
+            return pool.tile(shape, dtype, name=name, tag=tag or name, align_bytes=64)
 
         offsets = sb("offsets", [P, S // 16], U16)
         words = sb("words", [P, T], U32)
         scales = sb("scales", [P, T], U8)
-        raw = {k: sb("raw_" + k, [P, 4, N], F32) for k in ("q", "p", "f")}
+        raw = {k: sb("raw_" + k, [P, PACK, N], F32) for k in ("b", "a", "f")}
         seen = sb("seen", [P, BLOCKS, D], F32)
 
+        def load_weight(k, w):
+            nc.sync.dma_start(out=raw[k][:], in_=w.rearrange("(p j) n -> p j n", j=PACK))
+
+        nc.vector.memset(scales[:].bitcast(I32), 0)
         nc.sync.dma_start(offsets[:], offs)
+        load_weight("b", w3)
         scale_rows = x_scales[0].bitcast(I32)
         for q in range(4):
-            nc.sync.dma_start(
-                out=scales[32 * q : 32 * q + 32, :].bitcast(I32),
-                in_=scale_rows[4 * q : 4 * q + 4, :].unsqueeze(0).broadcast_to([8, 4, T // 4]),
-            )
+            nc.sync.dma_start(out=scales[32 * q : 32 * q + 4, :].bitcast(I32), in_=scale_rows[4 * q : 4 * q + 4, :])
         nc.sync.dma_start(out=words[:].bitcast(I32), in_=x_words[0].rearrange("p n t -> p (n t)").bitcast(I32))
-        for k, w in (("q", w3), ("p", w2), ("f", w1)):
-            nc.sync.dma_start(out=raw[k][:], in_=w.rearrange("(p j) n -> p j n", j=4))
+        load_weight("a", w2)
+        load_weight("f", w1)
         nc.sync.dma_start(out=seen[:], in_=vis[0:1, :].rearrange("o (b p d) -> p (o b) d", p=P, d=D))
-
-        warm = sb("warm", [P, 1], F32)
-        warm2 = sb("warm2", [P, 1], F32)
-        nc.vector.memset(warm[:], 0.0)
-        nc.scalar.activation(out=warm2[:], in_=warm[:], func=ACT.Sigmoid)
 
         ident = sb("ident", [P, P], F32)
         make_identity(nc, ident[:])
 
         x_codes = [sb("x_codes%d" % b, [P, BLOCK], U32) for b in range(BLOCKS)]
-        x_listed = [sb("x_listed%d" % b, [P, BLOCK], U8) for b in range(BLOCKS)]
         x_bytes = [sb("x_bytes%d" % b, [P, BLOCK], U8) for b in range(BLOCKS)]
-        w_bf = {k: sb("w_bf_" + k, [P, N, 4], BF16) for k in raw}
         w_codes = {k: sb("w_codes_" + k, [P, N], U32) for k in raw}
         w_bytes = {k: sb("w_bytes_" + k, [P, N], U8) for k in raw}
 
         def entries(b):
             return offsets[:, b * BLOCK // 16 : (b + 1) * BLOCK // 16]
 
-        def gather_bytes(b):
-            nc.vector.tensor_copy(x_listed[b][:], scales[:].indirect(entries(b)))
+        def gather_bytes(b, tag):
+            listed = sb("listed%d" % b, [P, BLOCK], U8, tag)
+            nc.vector.tensor_copy(listed[:], scales[:].indirect(entries(b)))
             nc.vector.tensor_copy(
-                x_bytes[b][:].rearrange("p (d v) -> p d v", d=D),
-                x_listed[b][:].rearrange("p (v d) -> p d v", d=D),
+                x_bytes[b][:].rearrange("p (d c i) -> p c d i", d=D, i=16),
+                listed[:].rearrange("p (c i d) -> p c d i", d=D, i=16),
             )
 
         def gather_words(b):
             nc.vector.tensor_copy(x_codes[b][:].rearrange("p (d v) -> p v d", d=D), words[:].indirect(entries(b)))
 
-        def views(k):
-            return (w_bf[k][:].rearrange("p (c i) t -> p c t i", i=4), raw[k][:].rearrange("p t (c i) -> p c t i", i=4))
-
-        def quantise(k):
+        def quantise(k, copy, tag):
+            rounded = sb("rounded_" + k, [P, N, PACK], BF16, tag)
+            copy(
+                out=rounded[:].rearrange("p (c i) t -> p c t i", i=4),
+                in_=raw[k][:].rearrange("p t (c i) -> p c t i", i=4),
+            )
             nc.vector.quantize_mx(
                 out=w_codes[k][:].bitcast(FP8X4),
                 scales=w_bytes[k][:],
-                in_=w_bf[k][:].rearrange("p n t -> p (n t)"),
+                in_=rounded[:].rearrange("p n t -> p (n t)"),
             )
 
-        banks = {(k, u): psum.tile([P, 2 * N], F32, name="bank_%s%d" % (k, u)) for k in ("p", "q") for u in range(4)}
-
         def product(k, u, bank):
-            b, h = UNITS[u]
             for i in range(2):
-                cols = slice((2 * h + i) * P, (2 * h + i + 1) * P)
+                b, d = divmod(2 * u + i, D)
+                cols = slice(d * P, (d + 1) * P)
                 nc.tensor.matmul_mx(
                     out=bank[:, i * N : (i + 1) * N],
                     lhsT=x_codes[b][:, cols].bitcast(FP8X4),
@@ -106,94 +105,87 @@ def tile_picked_ymisw_pow_p_kernel(tc, x_words, x_scales, w1, w2, w3, vis, offs,
                     stop=True,
                 )
 
-        sig = [sb("sig%d" % u, [P, 2, 2 * N], F32) for u in range(4)]
-        side = {"p": 0, "q": 1}
-
-        def sigmoid(k, u):
-            product(k, u, banks[k, u])
-            nc.scalar.activation(out=sig[u][:, side[k], :], in_=banks[k, u][:], func=ACT.Sigmoid)
-
-        gather_bytes(0)
-        gather_bytes(1)
+        gather_bytes(0, None)
+        quantise("b", nc.scalar.copy, None)
         gather_words(0)
-        dst, src = views("q")
-        nc.scalar.activation(out=dst, in_=src, func=ACT.Copy, scale=-1.0)
-        quantise("q")
-        dst, src = views("p")
-        nc.vector.tensor_scalar(out=dst, in0=src, scalar1=-1.0, scalar2=None, op0=ALU.mult)
-        sigmoid("q", 0)
-        sigmoid("q", 1)
-        quantise("p")
         gather_words(1)
-        sigmoid("p", 0)
-        sigmoid("p", 1)
-        for u in (2, 3):
-            sigmoid("q", u)
-        for u in (2, 3):
-            sigmoid("p", u)
-        dst, src = views("f")
-        nc.vector.tensor_copy(out=dst, in_=src)
-        quantise("f")
+        quantise("a", nc.scalar.copy, "late")
+        gather_bytes(1, "late")
+        quantise("f", nc.vector.tensor_copy, "late")
 
-        logs = [sb("logs%d" % u, [P, 2, 2 * N], F32) for u in range(4)]
-        neg_a = sb("neg_a", [P, 8, N], F32)
-        neg_b = [sb("neg_b%d" % u, [P, 2 * N], F32) for u in range(4)]
-        sq_a = [sb("sq_a%d" % u, [P, 2 * N], F32) for u in range(4)]
-        sq_b = [sb("sq_b%d" % u, [P, 2 * N], F32) for u in range(4)]
-        den = [sb("den%d" % u, [P, 2 * N], F32) for u in range(4)]
-        log_den = [sb("log_den%d" % u, [P, 2 * N], F32) for u in range(4)]
-        expo = sb("expo", [P, 8, N], F32)
+        banks = {(u, k): psum.tile([P, 2 * N], F32, name="bank%d%s" % (u, k)) for u in range(PAIRS) for k in SIDES}
+        grown = [sb("grown%d" % b, [P, 2, 2, 2 * N], F32, "raw_a" if b == 0 else None) for b in range(BLOCKS)]
+        capped = [sb("capped%d" % u, [P, 2, 2 * N], F32) for u in range(PAIRS)]
+        for b in range(BLOCKS):
+            for s, k in enumerate(SIDES):
+                for u in (2 * b, 2 * b + 1):
+                    product(k, u, banks[u, k])
+                    nc.scalar.activation(out=grown[b][:, u % 2, s, :], in_=banks[u, k][:], func=ACT.Exp)
+            for u in (2 * b, 2 * b + 1):
+                nc.vector.tensor_scalar(out=capped[u][:], in0=grown[b][:, u % 2, :, :], scalar1=CAP, scalar2=None, op0=ALU.min)
 
-        def unit(t, u):
-            return t[:, 2 * u : 2 * u + 2, :].rearrange("p i n -> p (i n)")
+        logs = [sb("logs%d" % u, [P, 2, 2 * N], F32) for u in range(PAIRS)]
+        pdf = {(u, k): sb("pdf%d%s" % (u, k), [P, 2, N], F32) for u in range(PAIRS) for k in SIDES}
+        for u in range(PAIRS):
+            for part in (slice(0, 1), slice(1, 2)) if u == 0 else (slice(0, 2),):
+                nc.scalar.activation(out=logs[u][:, part, :], in_=capped[u][:, part, :], func=ACT.Ln, scale=GAIN, bias=GAIN)
+        for u in range(PAIRS):
+            for s, k in enumerate(SIDES):
+                nc.vector.scalar_tensor_tensor(
+                    out=pdf[u, k][:].rearrange("p i n -> p (i n)"),
+                    in0=banks[u, k][:],
+                    scalar=FLOOR,
+                    in1=logs[u][:, s, :],
+                    op0=ALU.add,
+                    op1=ALU.max,
+                )
 
-        def stage_log(u):
-            c = math.e ** -FLOOR
-            nc.scalar.activation(out=logs[u][:], in_=sig[u][:], func=ACT.Ln, scale=c, bias=c * TINY)
+        log_den = [sb("log_den%d" % u, [P, 2, N], F32) for u in range(PAIRS)]
+        for u in range(PAIRS):
+            product("f", u, banks[u, "a"])
+            square = {k: sb("square%d%s" % (u, k), [P, 2, N], F32) for k in SIDES}
+            for k in SIDES:
+                if u >= PAIRS // 2:
+                    nc.scalar.activation(out=square[k][:], in_=pdf[u, k][:], func=ACT.Square)
+                else:
+                    engine = nc.vector if (u, k) == (0, SIDES[0]) else nc.gpsimd
+                    engine.tensor_tensor(out=square[k][:], in0=pdf[u, k][:], in1=pdf[u, k][:], op=ALU.mult)
+            den = sb("den%d" % u, [P, 2, N], F32)
+            nc.vector.tensor_tensor(out=den[:], in0=square["a"][:], in1=square["b"][:], op=ALU.add)
+            nc.scalar.activation(out=log_den[u][:], in_=den[:], func=ACT.Ln)
 
-        def stage_min(u):
+        power = sb("power", [P, PAIRS, 2, N], F32)
+        for u in range(PAIRS):
             nc.vector.scalar_tensor_tensor(
-                out=neg_b[u][:], in0=banks["q", u][:], scalar=-FLOOR, in1=logs[u][:, 1, :], op0=ALU.add, op1=ALU.min
-            )
-            nc.vector.scalar_tensor_tensor(
-                out=unit(neg_a, u), in0=banks["p", u][:], scalar=-FLOOR, in1=logs[u][:, 0, :], op0=ALU.add, op1=ALU.min
-            )
-            product("f", u, banks["p", u])
-
-        def stage_den(u):
-            nc.scalar.activation(out=sq_b[u][:], in_=neg_b[u][:], func=ACT.Square)
-            nc.vector.tensor_tensor(out=sq_a[u][:], in0=unit(neg_a, u), in1=unit(neg_a, u), op=ALU.mult)
-            nc.vector.tensor_tensor(out=den[u][:], in0=sq_a[u][:], in1=sq_b[u][:], op=ALU.add)
-
-        def stage_expo(u):
-            nc.scalar.activation(out=log_den[u][:], in_=den[u][:], func=ACT.Ln)
-            nc.vector.scalar_tensor_tensor(
-                out=unit(expo, u), in0=banks["p", u][:], scalar=0.6, in1=log_den[u][:], op0=ALU.mult, op1=ALU.subtract
+                out=power[:, u, :, :].rearrange("p i n -> p (i n)"),
+                in0=banks[u, "a"][:],
+                scalar=0.6,
+                in1=log_den[u][:].rearrange("p i n -> p (i n)"),
+                op0=ALU.mult,
+                op1=ALU.subtract,
             )
 
-        stages = (stage_log, stage_min, stage_den, stage_expo)
-        for step in range(4 + len(stages) - 1):
-            for s, stage in enumerate(stages):
-                if 0 <= step - s < 4:
-                    stage(step - s)
-
-        for m in range(2):
+        for m in range(N // P):
             cols = slice(m * P, (m + 1) * P)
-            result = sb("result%d" % m, [P, BLOCKS, P], F32)
-            for c in range(2):
-                ratio = sb("ratio%d%d" % (m, c), [P, 4, P], F32)
-                est = sb("est%d%d" % (m, c), [P, 4, P], F32)
-                nc.scalar.activation(out=ratio[:], in_=expo[:, c:8:2, cols], func=ACT.Exp)
-                for u, (b, h) in enumerate(UNITS):
-                    d = 2 * h + c
+            sums = [banks[BLOCKS * m + b, "b"][:, 0:P] for b in range(BLOCKS)]
+            for i in range(2):
+                ratio = sb("ratio%d%d" % (m, i), [P, PAIRS, P], F32)
+                est = sb("est%d%d" % (m, i), [P, PAIRS, P], F32)
+                nc.scalar.activation(out=ratio[:], in_=power[:, :, i, cols], func=ACT.Exp)
+                for u in range(PAIRS):
+                    b, d = divmod(2 * u + i, D)
                     nc.vector.scalar_tensor_tensor(
-                        out=est[:, u, :], in0=ratio[:, u, :], scalar=seen[:, b, d : d + 1], in1=neg_a[:, 2 * u + c, cols],
-                        op0=ALU.mult, op1=ALU.mult,
+                        out=est[:, u, :],
+                        in0=ratio[:, u, :],
+                        scalar=seen[:, b, d : d + 1],
+                        in1=pdf[u, "a"][:, i, cols],
+                        op0=ALU.mult,
+                        op1=ALU.mult,
                     )
                     nc.tensor.matmul(
-                        banks["q", 2 * m + b][:, 0:P], lhsT=est[:, u, :], rhs=ident[:],
-                        start=(c == 0 and h == 0), stop=(c == 1 and h == 1), is_transpose=True,
+                        sums[b], lhsT=est[:, u, :], rhs=ident[:], start=(d == 0), stop=(d == D - 1), is_transpose=True
                     )
             for b in range(BLOCKS):
-                nc.scalar.activation(out=result[:, b, :], in_=banks["q", 2 * m + b][:, 0:P], func=ACT.Copy, scale=-1.0 / D)
-            nc.sync.dma_start(out=out[cols, :], in_=result[:].rearrange("p b v -> p (b v)"))
+                mean = sb("mean%d%d" % (m, b), [P, P], F32)
+                nc.scalar.activation(out=mean[:], in_=sums[b], func=ACT.Copy, scale=1.0 / D)
+                nc.sync.dma_start(out=out[cols, b * P : (b + 1) * P], in_=mean[:])

import math
from contextlib import ExitStack

import concourse.mybir as mybir
from concourse.masks import make_identity

K, T, S, D, N = 512, 2048, 1024, 4, 256
P = 128
FLOPS = 3 * 2 * K * N * S

F32 = mybir.dt.float32
BF16 = mybir.dt.bfloat16
I32 = mybir.dt.int32
U32 = mybir.dt.uint32
U16 = mybir.dt.uint16
U8 = mybir.dt.uint8
FP8X4 = mybir.dt.float8_e4m3fn_x4
ACT = mybir.ActivationFunctionType
ALU = mybir.AluOpType

PACK = 4
BLOCK = P * D
BLOCKS = S // BLOCK
PAIRS = S // (2 * P)
SIDES = ("b", "a")
FLOOR = 0.2
GAIN = math.e**FLOOR
CAP = 2.0**60


def tile_picked_ymisw_pow_p_kernel(tc, x_words, x_scales, w1, w2, w3, vis, offs, out):
    nc = tc.nc
    with ExitStack() as ctx:
        pool = ctx.enter_context(tc.tile_pool(name="sbuf", bufs=1))
        psum = ctx.enter_context(tc.psum_pool(name="psum", bufs=1))

        def sb(name, shape, dtype, tag=None):
            return pool.tile(shape, dtype, name=name, tag=tag or name, align_bytes=64)

        offsets = sb("offsets", [P, S // 16], U16)
        words = sb("words", [P, T], U32)
        scales = sb("scales", [P, T], U8)
        raw = {k: sb("raw_" + k, [P, PACK, N], F32) for k in ("b", "a", "f")}
        seen = sb("seen", [P, BLOCKS, D], F32)

        def load_weight(k, w):
            nc.sync.dma_start(out=raw[k][:], in_=w.rearrange("(p j) n -> p j n", j=PACK))

        nc.vector.memset(scales[:].bitcast(I32), 0)
        nc.sync.dma_start(offsets[:], offs)
        load_weight("b", w3)
        scale_rows = x_scales[0].bitcast(I32)
        for q in range(4):
            nc.sync.dma_start(out=scales[32 * q : 32 * q + 4, :].bitcast(I32), in_=scale_rows[4 * q : 4 * q + 4, :])
        nc.sync.dma_start(out=words[:].bitcast(I32), in_=x_words[0].rearrange("p n t -> p (n t)").bitcast(I32))
        load_weight("a", w2)
        load_weight("f", w1)
        nc.sync.dma_start(out=seen[:], in_=vis[0:1, :].rearrange("o (b p d) -> p (o b) d", p=P, d=D))

        ident = sb("ident", [P, P], F32)
        make_identity(nc, ident[:])

        x_codes = [sb("x_codes%d" % b, [P, BLOCK], U32) for b in range(BLOCKS)]
        x_bytes = [sb("x_bytes%d" % b, [P, BLOCK], U8) for b in range(BLOCKS)]
        w_codes = {k: sb("w_codes_" + k, [P, N], U32) for k in raw}
        w_bytes = {k: sb("w_bytes_" + k, [P, N], U8) for k in raw}

        def entries(b):
            return offsets[:, b * BLOCK // 16 : (b + 1) * BLOCK // 16]

        def gather_bytes(b, tag):
            listed = sb("listed%d" % b, [P, BLOCK], U8, tag)
            nc.vector.tensor_copy(listed[:], scales[:].indirect(entries(b)))
            nc.vector.tensor_copy(
                x_bytes[b][:].rearrange("p (d c i) -> p c d i", d=D, i=16),
                listed[:].rearrange("p (c i d) -> p c d i", d=D, i=16),
            )

        def gather_words(b):
            nc.vector.tensor_copy(x_codes[b][:].rearrange("p (d v) -> p v d", d=D), words[:].indirect(entries(b)))

        def quantise(k, copy, tag):
            rounded = sb("rounded_" + k, [P, N, PACK], BF16, tag)
            copy(
                out=rounded[:].rearrange("p (c i) t -> p c t i", i=4),
                in_=raw[k][:].rearrange("p t (c i) -> p c t i", i=4),
            )
            nc.vector.quantize_mx(
                out=w_codes[k][:].bitcast(FP8X4),
                scales=w_bytes[k][:],
                in_=rounded[:].rearrange("p n t -> p (n t)"),
            )

        def product(k, u, bank):
            for i in range(2):
                b, d = divmod(2 * u + i, D)
                cols = slice(d * P, (d + 1) * P)
                nc.tensor.matmul_mx(
                    out=bank[:, i * N : (i + 1) * N],
                    lhsT=x_codes[b][:, cols].bitcast(FP8X4),
                    lhsT_scale=x_bytes[b][:, cols],
                    rhs=w_codes[k][:].bitcast(FP8X4),
                    rhs_scale=w_bytes[k][:],
                    start=True,
                    stop=True,
                )

        gather_bytes(0, None)
        quantise("b", nc.scalar.copy, None)
        gather_words(0)
        gather_words(1)
        quantise("a", nc.scalar.copy, "late")
        gather_bytes(1, "late")
        quantise("f", nc.vector.tensor_copy, "late")

        banks = {(u, k): psum.tile([P, 2 * N], F32, name="bank%d%s" % (u, k)) for u in range(PAIRS) for k in SIDES}
        grown = [sb("grown%d" % b, [P, 2, 2, 2 * N], F32, "raw_a" if b == 0 else None) for b in range(BLOCKS)]
        capped = [sb("capped%d" % u, [P, 2, 2 * N], F32) for u in range(PAIRS)]
        for b in range(BLOCKS):
            for s, k in enumerate(SIDES):
                for u in (2 * b, 2 * b + 1):
                    product(k, u, banks[u, k])
                    nc.scalar.activation(out=grown[b][:, u % 2, s, :], in_=banks[u, k][:], func=ACT.Exp)
            for u in (2 * b, 2 * b + 1):
                nc.vector.tensor_scalar(out=capped[u][:], in0=grown[b][:, u % 2, :, :], scalar1=CAP, scalar2=None, op0=ALU.min)

        logs = [sb("logs%d" % u, [P, 2, 2 * N], F32) for u in range(PAIRS)]
        pdf = {(u, k): sb("pdf%d%s" % (u, k), [P, 2, N], F32) for u in range(PAIRS) for k in SIDES}
        for u in range(PAIRS):
            for part in (slice(0, 1), slice(1, 2)) if u == 0 else (slice(0, 2),):
                nc.scalar.activation(out=logs[u][:, part, :], in_=capped[u][:, part, :], func=ACT.Ln, scale=GAIN, bias=GAIN)
        for u in range(PAIRS):
            for s, k in enumerate(SIDES):
                nc.vector.scalar_tensor_tensor(
                    out=pdf[u, k][:].rearrange("p i n -> p (i n)"),
                    in0=banks[u, k][:],
                    scalar=FLOOR,
                    in1=logs[u][:, s, :],
                    op0=ALU.add,
                    op1=ALU.max,
                )

        log_den = [sb("log_den%d" % u, [P, 2, N], F32) for u in range(PAIRS)]
        for u in range(PAIRS):
            product("f", u, banks[u, "a"])
            square = {k: sb("square%d%s" % (u, k), [P, 2, N], F32) for k in SIDES}
            for k in SIDES:
                if u >= PAIRS // 2:
                    nc.scalar.activation(out=square[k][:], in_=pdf[u, k][:], func=ACT.Square)
                else:
                    engine = nc.vector if (u, k) == (0, SIDES[0]) else nc.gpsimd
                    engine.tensor_tensor(out=square[k][:], in0=pdf[u, k][:], in1=pdf[u, k][:], op=ALU.mult)
            den = sb("den%d" % u, [P, 2, N], F32)
            nc.vector.tensor_tensor(out=den[:], in0=square["a"][:], in1=square["b"][:], op=ALU.add)
            nc.scalar.activation(out=log_den[u][:], in_=den[:], func=ACT.Ln)

        power = sb("power", [P, PAIRS, 2, N], F32)
        for u in range(PAIRS):
            nc.vector.scalar_tensor_tensor(
                out=power[:, u, :, :].rearrange("p i n -> p (i n)"),
                in0=banks[u, "a"][:],
                scalar=0.6,
                in1=log_den[u][:].rearrange("p i n -> p (i n)"),
                op0=ALU.mult,
                op1=ALU.subtract,
            )

        for m in range(N // P):
            cols = slice(m * P, (m + 1) * P)
            sums = [banks[BLOCKS * m + b, "b"][:, 0:P] for b in range(BLOCKS)]
            for i in range(2):
                ratio = sb("ratio%d%d" % (m, i), [P, PAIRS, P], F32)
                est = sb("est%d%d" % (m, i), [P, PAIRS, P], F32)
                nc.scalar.activation(out=ratio[:], in_=power[:, :, i, cols], func=ACT.Exp)
                for u in range(PAIRS):
                    b, d = divmod(2 * u + i, D)
                    nc.vector.scalar_tensor_tensor(
                        out=est[:, u, :],
                        in0=ratio[:, u, :],
                        scalar=seen[:, b, d : d + 1],
                        in1=pdf[u, "a"][:, i, cols],
                        op0=ALU.mult,
                        op1=ALU.mult,
                    )
                    nc.tensor.matmul(
                        sums[b], lhsT=est[:, u, :], rhs=ident[:], start=(d == 0), stop=(d == D - 1), is_transpose=True
                    )
            for b in range(BLOCKS):
                mean = sb("mean%d%d" % (m, b), [P, P], F32)
                nc.scalar.activation(out=mean[:], in_=sums[b], func=ACT.Copy, scale=1.0 / D)
                nc.sync.dma_start(out=out[cols, b * P : (b + 1) * P], in_=mean[:])
